import numpy as np, ml_dtypes
CORES = [51,54,179,182]
N = 4
J, Q = 256, 2048
def entries(a): return a.T.reshape(-1)
def pack(v, P): return np.ascontiguousarray(np.asarray(v, np.int32).reshape(-1, P).T)
def split(rng, total, parts):
    c = np.sort(rng.integers(0, total + 1, parts - 1)); return np.diff(np.concatenate([[0], c, [total]]))
def lists(rng, how):
    s = np.concatenate([[0], rng.integers(1 - Q // 2, Q // 2 + 1, N - 1), [int(rng.integers(1 - Q // 2, 1))]])
    if how == "early": s[1:] = -Q; s[N] = -2 * Q
    if how == "late": s[1:] = Q; s[N] = 0
    if how == "long":
        z = int(rng.integers(1, N - 1)); s[1:z] = -rng.integers(1, Q, z - 1); s[z] = -Q; s[z + 1] = Q; s[z + 2:N] = rng.integers(1, Q, N - z - 2); s[N] = -int(rng.integers(0, Q - s[N - 1] + 1))
    if how == "sway":
        z = int(rng.integers(1, N - 2)); e = int(rng.integers(z + 1, N - 1)); s[1:] = -rng.integers(Q // 2 + 1, Q, N); s[z + 1:e + 1] = rng.integers(Q // 2 + 1, Q - 1, e - z); s[e + 1] = s[e] - Q; s[N] = s[N - 1] - Q + int(rng.integers(1, -s[N - 1]))
    tot = Q + np.diff(s)
    L = np.stack([split(rng, int(t), J) for t in tot])
    if how == "gaps":
        L = np.zeros((N, J), np.int64)
        for r in range(N): m = 1 if r & 1 else 8; L[r, 1 + rng.permutation(J - 2)[:m]] = split(rng, int(tot[r]), m)
    if how == "long":
        L = np.zeros((N, J), np.int64); L[np.arange(N), rng.integers(0, J, N)] = tot
    return {"ln": np.stack([pack(l, 16) for l in L])}
def setup_inputs(rng):
    return dict({"x": rng.standard_normal((N, 128, J), dtype=np.float32).astype(ml_dtypes.bfloat16)}, **lists(rng, "uniform"))
def setup_inputs_early(rng):
    d = setup_inputs(rng); d.update(lists(rng, "early"))
    for k in ("x",): d[k] = (d[k].astype(np.float32) * 1048576.0).astype(d[k].dtype)
    return d
def setup_inputs_gaps(rng):
    d = setup_inputs(rng); d.update(lists(rng, "gaps"))
    for k in ("x",): d[k] = (d[k].astype(np.float32) * (1 / 1024.0)).astype(d[k].dtype)
    return d
def setup_inputs_late(rng):
    d = setup_inputs(rng); d.update(lists(rng, "late"))
    return d
def setup_inputs_long(rng):
    d = setup_inputs(rng); d.update(lists(rng, "long"))
    return d
def setup_inputs_sway(rng):
    d = setup_inputs(rng); d.update(lists(rng, "sway"))
    return d
def check_inputs(x):
    bad = []
    if x["ln"].min() < 0 or x["ln"].max() >= N * Q + 1: bad.append("ln out of range")
    if int(x["ln"].sum()) > N * Q: bad.append("the lengths come to more than N * Q")
    c = np.concatenate([[0], np.cumsum([int(a.sum()) for a in x["ln"]])])
    if any(c[r] < (r - 1) * Q or c[r + 1] > (r + 2) * Q for r in range(N)): bad.append("the sums of the lengths before or up to a rank leave their bounds")
    return bad
def reference(x, ln):
    got = np.concatenate([np.repeat(x[r], entries(ln[r]), axis=1) for r in range(N)], axis=1)[:, :N * Q]
    Y = np.zeros((128, N * Q), x.dtype); Y[:, :got.shape[1]] = got
    return {"y": np.stack([Y[:, Q * r:Q * r + Q] for r in range(N)])}

@@ -1,0 +1,225 @@
+from concourse.bass import DstId, RemoteDMATransfer
+from concourse.mybir import dt, AluOpType, AxisListType, ActivationFunctionType
+
+J, Q = 256, 2048
+NC = 34
+SCRATCH = {
+    "lnd": ("sbuf", [128, 8], "int32"),
+    "win": ("sbuf", [128, 3 * J + 8], "bfloat16"),
+    "off": ("sbuf", [128, Q // 16], "uint16"),
+    "yb": ("sbuf", [128, Q], "bfloat16"),
+    "ramp": ("sbuf", [128, 132], "int32"),
+    "mrow": ("sbuf", [128, 128], "int32"),
+    "colp": ("sbuf", [128, 4], "int32"),
+    "cola": ("sbuf", [128, 4], "int32"),
+    "colw": ("sbuf", [128, 4], "float32"),
+    "colj": ("sbuf", [128, 4], "float32"),
+    "colk": ("sbuf", [128, 4], "float32"),
+    "rowj": ("sbuf", [128, 128], "float32"),
+    "rowc": ("sbuf", [128, 136], "bfloat16"),
+    "rowa": ("sbuf", [128, 128], "bfloat16"),
+    "wd": ("sbuf", [128, 128], "bfloat16"),
+    "wup": ("sbuf", [128, 128], "bfloat16"),
+    "wdn": ("sbuf", [128, 128], "bfloat16"),
+    "ones": ("sbuf", [128, 128], "bfloat16"),
+    "zer": ("sbuf", [128, 8], "bfloat16"),
+    "csta": ("sbuf", [128, 8], "bfloat16"),
+    "cstb": ("sbuf", [128, 8], "bfloat16"),
+    "neg0": ("sbuf", [128, 4], "float32"),
+    "hi": ("sbuf", [128, 8], "bfloat16"),
+    "lo": ("sbuf", [128, 8], "bfloat16"),
+    "rhi": ("sbuf", [128, 16], "bfloat16"),
+    "rlo": ("sbuf", [128, 16], "bfloat16"),
+    "nps": ("sbuf", [128, 8], "float32"),
+    "e16": ("sbuf", [128, 8], "float32"),
+    "ca": ("sbuf", [128, 6 * 136], "bfloat16"),
+    "aa": ("sbuf", [128, 6 * 128], "bfloat16"),
+    "ab": ("sbuf", [128, 6 * 128], "bfloat16"),
+    "pe": ("psum", [128, 512], "float32"),
+    "pi": ("psum", [128, 512], "float32"),
+}
+SEMAPHORES = (["ldl", "ldx", "loc", "sty", "stz"] + ["la%d" % s for s in range(4)] + ["xa%d" % s for s in range(4)]
+              + ["e%d" % k for k in range(NC)])
+
+
+def window(r, n):
+    return max(0, r - 1), min(n, r + 2)
+
+
+def rank_program(g, core, T, topo):
+    r = T.rank_of(core)
+    if r is None:
+        return
+    n = len(T.cores)
+    A = AluOpType
+    AF = ActivationFunctionType
+    V, S, PE, Y = g.vector, g.scalar, g.tensor, g.sync
+    s0, s1 = window(r, n)
+    ns, nl = s1 - s0, s1
+    nt = 2 * ns
+    wlen = J * ns + 8
+    used = [0]
+
+    def ev():
+        used[0] += 1
+        return T.sem["e%d" % (used[0] - 1)]
+
+    Y.dma_start(T.lnd[:, 2 * r:2 * r + 2], T.ln[:]).then_inc(T.sem.ldl, 16)
+    xs = slice(J * (r - s0), J * (r - s0) + J)
+    S.dma_start(T.win[:, xs], T.x[:]).then_inc(T.sem.ldx, 16)
+
+    def same_chip(d):
+        return topo.host(d) == topo.host(core) and topo.chip(d) == topo.chip(core)
+
+    far = [d for d in range(n) if d != r and not same_chip(T.cores[d])]
+    near = [d for d in range(n) if d != r and same_chip(T.cores[d])]
+    ln_to = [d for d in range(n) if d != r and r < window(d, n)[1]]
+    x_to = [d for d in range(n) if d != r and window(d, n)[0] <= r < window(d, n)[1]]
+    offm = topo.mask(core, T.cores[far[0]])
+    onm = topo.mask(core, T.cores[near[0]]) & ~offm
+    cnt = {offm: bin(offm).count("1"), onm: bin(onm).count("1")}
+
+    def engines(src, dst):
+        return offm if dst in [d for d in range(n) if not (topo.host(T.cores[d]) == topo.host(T.cores[src])
+                    and topo.chip(T.cores[d]) == topo.chip(T.cores[src]))] else onm
+
+    def ident(d):
+        rid, pid = topo.addr(T.cores[d], core)
+        return DstId(rid=rid, pnc=pid)
+
+    sio = ev()
+    g.iota(T.colp[:, 0:1], [[1, 1]], 0, 1).then_inc(sio, 1)
+    g.iota(T.colw[:, 0:1], [[1, 1]], 0, 32, allow_small_or_imprecise_dtypes=True).then_inc(sio, 1)
+    g.iota(T.rowj[:], [[1, 16], [32, 8]], 0, 0, allow_small_or_imprecise_dtypes=True).then_inc(sio, 1)
+    g.iota(T.ramp[:, 0:129], [[1, 129]], 0, 0).then_inc(sio, 1)
+
+    nloc = 0
+    g.wait_ge(T.sem.ldl, 16)
+    lsl = T.lnd[:, 2 * r:2 * r + 2]
+    for mask, group in ((offm, [d for d in ln_to if d in far]), (onm, [d for d in ln_to if d in near])):
+        if group:
+            g.remote_dma_fused([RemoteDMATransfer(dst_ids=[ident(d) for d in group], dma_engine_mask=mask,
+                                                  remote_sem=T.sem["la%d" % r], srcs=[lsl], dsts=[lsl for d in group])],
+                               local_sem=T.sem.loc)
+            nloc += cnt[mask]
+    g.wait_ge(T.sem.ldx, 16)
+    trs = []
+    for d in x_to:
+        mask = offm if d in far else onm
+        a = J * (r - window(d, n)[0])
+        trs.append(RemoteDMATransfer(dst_ids=[ident(d)], dma_engine_mask=mask, remote_sem=T.sem["xa%d" % r],
+                                     srcs=[T.win[:, xs]], dsts=[T.win[:, a:a + J]]))
+        nloc += cnt[mask]
+    g.remote_dma_fused(trs, local_sem=T.sem.loc)
+    g.wait_ge(T.sem.loc, nloc)
+
+    sms, nms = ev(), 0
+    for ap, val in ((T.ones[:], 1.0), (T.zer[:], 0.0), (T.csta[:], -float(Q * r)), (T.cstb[:], -7.5), (T.neg0[:], -0.0),
+                    (T.rhi[:], 0.0), (T.rlo[:], 0.0), (T.win[:, J * ns:J * ns + 8], 0.0)):
+        V.memset(ap, val).then_inc(sms, 1)
+        nms += 1
+    V.wait_ge(sio, 4)
+    sc1, sc2, sc3, sw = ev(), ev(), ev(), ev()
+    V.tensor_scalar(T.cola[:, 0:1], T.colp[:, 0:1], 3, None, A.arith_shift_right).then_inc(sc1, 1)
+    V.tensor_scalar(T.mrow[:], T.ramp[:, 0:128], 15, None, A.bitwise_and).then_inc(sc1, 1)
+    srow = ev()
+    V.tensor_scalar(T.rowc[:, 0:129], T.ramp[:, 0:129], 16.0, -8.0, A.mult, A.add).then_inc(srow, 1)
+    V.wait_ge(sc1, 2)
+    V.tensor_scalar(T.colj[:, 0:1], T.cola[:, 0:1], -255.0, T.colw[:, 0:1], A.mult, A.add).then_inc(sc2, 1)
+    V.tensor_scalar(T.rowa[:], T.mrow[:], -7.0, None, A.add).then_inc(sc3, 1)
+    V.wait_ge(sc2, 1)
+    sc4 = ev()
+    V.tensor_scalar(T.colk[:, 0:1], T.colj[:, 0:1], -16.0, None, A.add).then_inc(sc4, 1)
+    V.tensor_scalar(T.wd[:], T.rowj[:], T.colj[:, 0:1], None, A.is_ge).then_inc(sw, 1)
+    V.tensor_scalar(T.wup[:], T.rowj[:], -16.0, T.colj[:, 0:1], A.add, A.is_ge).then_inc(sw, 1)
+    V.wait_ge(sc4, 1)
+    V.tensor_scalar(T.wdn[:], T.rowj[:], T.colk[:, 0:1], -1.0, A.is_lt, A.mult).then_inc(sw, 1)
+    V.wait_ge(sms, nms)
+    V.wait_ge(sc3, 1)
+
+    E = T.pe[:, 0:nt]
+    PE.wait_ge(sms, nms)
+    PE.matmul(E, T.ones[0:1, :], T.csta[0:1, 0:nt], True, False)
+    PE.matmul(E, T.ones[0:1, :], T.cstb[0:1, 0:nt], False, False)
+    PE.wait_ge(sw, 3)
+
+    V.wait_ge(T.sem.ldl, 16)
+    for s in range(nl):
+        if s != r:
+            V.wait_ge(T.sem["la%d" % s], cnt[engines(s, r)])
+    m64 = 1.5 * 2.0 ** 29
+    shi, slo, srh, srl = ev(), ev(), ev(), ev()
+    k = 2 * nl
+    V.tensor_scalar(T.hi[:, 0:k], T.lnd[:, 0:k], m64, m64, A.add, A.subtract).then_inc(shi, 1)
+    V.wait_ge(shi, 1)
+    V.tensor_tensor(T.lo[:, 0:k], T.lnd[:, 0:k], T.hi[:, 0:k], A.subtract).then_inc(slo, 1)
+    V.tensor_tensor_scan(T.rhi[:, 1:k], T.zer[:, 0:k - 1], T.hi[:, 0:k - 1], 0.0, A.add, A.add).then_inc(srh, 1)
+    V.wait_ge(slo, 1)
+    V.tensor_tensor_scan(T.rlo[:, 1:k], T.zer[:, 0:k - 1], T.lo[:, 0:k - 1], 0.0, A.add, A.add).then_inc(srl, 1)
+
+    lo0, hi0 = 2 * s0, 2 * s1
+    sE = ev()
+    for sm, t in ((shi, T.hi), (slo, T.lo)):
+        PE.wait_ge(sm, 1)
+        PE.matmul(E, T.wd[:], t[:, lo0:hi0], False, False)
+        PE.matmul(T.pe[:, 0:nt:2], T.wup[:], t[:, lo0 + 1:hi0:2], False, False)
+        PE.matmul(T.pe[:, 1:nt:2], T.wdn[:], t[:, lo0:hi0:2], False, False)
+    PE.wait_ge(srh, 1)
+    PE.matmul(E, T.ones[:], T.rhi[:, lo0:hi0], False, False)
+    PE.wait_ge(srl, 1)
+    PE.matmul(E, T.ones[:], T.rlo[:, lo0:hi0], False, True).then_inc(sE, 1)
+
+    m16 = 1.5 * 2.0 ** 27
+    snp, s16 = ev(), ev()
+    V.wait_ge(sE, 1)
+    V.tensor_scalar(T.nps[:, 0:nt], E, -1.0, None, A.mult).then_inc(snp, 1)
+    V.tensor_scalar(T.e16[:, 0:nt], E, m16, m16, A.add, A.subtract).then_inc(s16, 1)
+    V.wait_ge(s16, 1)
+    S.wait_ge(srow, 1)
+    S.wait_ge(sms, nms)
+    S.wait_ge(snp, 1)
+    stile = [ev() for i in range(nt)]
+    for i in range(nt):
+        b = slice(128 * i, 128 * i + 128)
+        S.activation(T.ca[:, 136 * i:136 * i + 129], T.rowc[:, 0:129], AF.Sign, bias=T.nps[:, i:i + 1]).then_inc(stile[i], 1)
+        V.tensor_scalar(T.aa[:, b], T.rowa[:], T.e16[:, i:i + 1], T.pe[:, i:i + 1], A.add, A.is_ge).then_inc(stile[i], 1)
+        V.tensor_scalar(T.ab[:, b], T.rowa[:], T.e16[:, i:i + 1], T.pe[:, i:i + 1], A.add, A.is_lt).then_inc(stile[i], 1)
+
+    spi = ev()
+    for i in range(nt):
+        b = slice(128 * i, 128 * i + 128)
+        PE.wait_ge(stile[i], 3)
+        PE.matmul(T.pi[:, 0:128], T.aa[:, b], T.ca[:, 136 * i + 1:136 * i + 129], i == 0, False)
+        last = PE.matmul(T.pi[:, 0:128], T.ab[:, b], T.ca[:, 136 * i:136 * i + 128], False, i == nt - 1)
+    last.then_inc(spi, 1)
+
+    V.wait_ge(spi, 1)
+    soa, sob = ev(), ev()
+    V.tensor_scalar(T.off[:, 64:128], T.pi[:, 64:128], float(128 * nt), 0.5, A.add, A.mult).then_inc(soa, 1)
+    V.tensor_scalar(T.off[:, 0:64], T.pi[:, 0:64], float(128 * nt), 0.5, A.add, A.mult).then_inc(sob, 1)
+    for q in (V, S):
+        q.wait_ge(T.sem.ldx, 16)
+        for s in range(s0, s1):
+            if s != r:
+                q.wait_ge(T.sem["xa%d" % s], cnt[engines(s, r)])
+    V.wait_ge(sob, 1)
+    S.wait_ge(soa, 1)
+    win = T.win[:, 0:wlen]
+    done = []
+    for c in range(2):
+        a = 512 * c
+        sv, ss = ev(), ev()
+        V.tensor_copy(T.yb[:, a:a + 512], win.indirect(T.off[:, a // 16:a // 16 + 32])).then_inc(sv, 1)
+        b = 1024 + 512 * c
+        S.activation(T.yb[:, b:b + 512], win.indirect(T.off[:, b // 16:b // 16 + 32]), AF.Identity,
+                     bias=T.neg0[:, 0:1]).then_inc(ss, 1)
+        done.append((a, sv))
+        done.append((b, ss))
+    for a, sm in done[:3]:
+        Y.wait_ge(sm, 1)
+        Y.dma_start(T.y[:, a:a + 512], T.yb[:, a:a + 512]).then_inc(T.sem.sty, 16)
+    a, sm = done[3]
+    S.wait_ge(sm, 1)
+    S.dma_start(T.y[:, a:a + 512], T.yb[:, a:a + 512]).then_inc(T.sem.stz, 16)
+    Y.wait_ge(T.sem.sty, 48)
+    S.wait_ge(T.sem.stz, 16)

@@ -2,22 +2,25 @@ from concourse.bass import DstId, RemoteDMATransfer
 from concourse.mybir import dt, AluOpType, AxisListType, ActivationFunctionType
 
 J, Q = 256, 2048
-NC = 34
+NC = 56
+BLOCKS = (256, 416, 352)
 SCRATCH = {
+    "lnx": ("dram", [128, 2], "int32"),
     "lnd": ("sbuf", [128, 8], "int32"),
+    "lnf": ("sbuf", [128, 8], "float32"),
     "win": ("sbuf", [128, 3 * J + 8], "bfloat16"),
     "off": ("sbuf", [128, Q // 16], "uint16"),
     "yb": ("sbuf", [128, Q], "bfloat16"),
-    "ramp": ("sbuf", [128, 132], "int32"),
-    "mrow": ("sbuf", [128, 128], "int32"),
     "colp": ("sbuf", [128, 4], "int32"),
     "cola": ("sbuf", [128, 4], "int32"),
     "colw": ("sbuf", [128, 4], "float32"),
     "colj": ("sbuf", [128, 4], "float32"),
     "colk": ("sbuf", [128, 4], "float32"),
-    "rowj": ("sbuf", [128, 128], "float32"),
+    "rowj": ("sbuf", [128, 128], "bfloat16"),
     "rowc": ("sbuf", [128, 136], "bfloat16"),
     "rowa": ("sbuf", [128, 128], "bfloat16"),
+    "eight": ("sbuf", [128, 136], "bfloat16"),
+    "semi": ("sbuf", [128, 16], "bfloat16"),
     "wd": ("sbuf", [128, 128], "bfloat16"),
     "wup": ("sbuf", [128, 128], "bfloat16"),
     "wdn": ("sbuf", [128, 128], "bfloat16"),
@@ -36,14 +39,22 @@ SCRATCH = {
     "aa": ("sbuf", [128, 6 * 128], "bfloat16"),
     "ab": ("sbuf", [128, 6 * 128], "bfloat16"),
     "pe": ("psum", [128, 512], "float32"),
-    "pi": ("psum", [128, 512], "float32"),
+    "pi0": ("psum", [128, 512], "float32"),
+    "pi1": ("psum", [128, 512], "float32"),
 }
-SEMAPHORES = (["ldl", "ldx", "loc", "sty", "stz"] + ["la%d" % s for s in range(4)] + ["xa%d" % s for s in range(4)]
+SEMAPHORES = (["ldl", "ldo", "ldx", "loc", "sty"] + ["la%d" % s for s in range(4)] + ["xa%d" % s for s in range(4)]
               + ["e%d" % k for k in range(NC)])
 
 
 def window(r, n):
     return max(0, r - 1), min(n, r + 2)
+
+
+def ln_dests(r, n):
+    ds = [d for d in range(n) if d != r and r < window(d, n)[1]]
+    size = {d: window(d, n)[1] - window(d, n)[0] for d in range(n)}
+    top = max(size.values())
+    return [d for d in ds if size[d] == top], [d for d in ds if size[d] < top]
 
 
 def rank_program(g, core, T, topo):
@@ -64,24 +75,40 @@ def rank_program(g, core, T, topo):
         used[0] += 1
         return T.sem["e%d" % (used[0] - 1)]
 
-    Y.dma_start(T.lnd[:, 2 * r:2 * r + 2], T.ln[:]).then_inc(T.sem.ldl, 16)
     xs = slice(J * (r - s0), J * (r - s0) + J)
-    S.dma_start(T.win[:, xs], T.x[:]).then_inc(T.sem.ldx, 16)
+    Y.dma_start(T.lnx[:], T.ln[:]).then_inc(T.sem.ldl, 16)
+    Y.dma_start(T.win[:, xs], T.x[:]).then_inc(T.sem.ldx, 16)
+    Y.dma_start(T.lnd[:, 2 * r:2 * r + 2], T.ln[:]).then_inc(T.sem.ldo, 16)
 
-    def same_chip(d):
-        return topo.host(d) == topo.host(core) and topo.chip(d) == topo.chip(core)
+    def is_near(a, b):
+        a, b = T.cores[a], T.cores[b]
+        return topo.host(a) == topo.host(b) and topo.chip(a) == topo.chip(b)
 
-    far = [d for d in range(n) if d != r and not same_chip(T.cores[d])]
-    near = [d for d in range(n) if d != r and same_chip(T.cores[d])]
-    ln_to = [d for d in range(n) if d != r and r < window(d, n)[1]]
-    x_to = [d for d in range(n) if d != r and window(d, n)[0] <= r < window(d, n)[1]]
-    offm = topo.mask(core, T.cores[far[0]])
-    onm = topo.mask(core, T.cores[near[0]]) & ~offm
-    cnt = {offm: bin(offm).count("1"), onm: bin(onm).count("1")}
+    def masks(s):
+        far = [d for d in range(n) if not is_near(s, d)][0]
+        near = [d for d in range(n) if d != s and is_near(s, d)][0]
+        m = topo.mask(T.cores[s], T.cores[far])
+        return m, topo.mask(T.cores[s], T.cores[near]) & ~m
 
-    def engines(src, dst):
-        return offm if dst in [d for d in range(n) if not (topo.host(T.cores[d]) == topo.host(T.cores[src])
-                    and topo.chip(T.cores[d]) == topo.chip(T.cores[src]))] else onm
+    def ln_calls(s):
+        offm, onm = masks(s)
+        first, rest = ln_dests(s, n)
+        calls = []
+        fars = [d for d in first if not is_near(s, d)]
+        nears = [d for d in first if is_near(s, d)]
+        calls.append([(offm if fars else onm, fars + nears)])
+        calls.append([(m, ds) for m, ds in ((offm, [d for d in rest if not is_near(s, d)]),
+                                            (onm, [d for d in rest if is_near(s, d)])) if ds])
+        return [c for c in calls if c]
+
+    def ones_of(m):
+        return bin(m).count("1")
+
+    def ln_count(s, d):
+        return [ones_of(m) for c in ln_calls(s) for m, ds in c if d in ds][0]
+
+    def x_mask(s, d):
+        return masks(s)[1 if is_near(s, d) else 0]
 
     def ident(d):
         rid, pid = topo.addr(T.cores[d], core)
@@ -89,53 +116,56 @@ def rank_program(g, core, T, topo):
 
     sio = ev()
     g.iota(T.colp[:, 0:1], [[1, 1]], 0, 1).then_inc(sio, 1)
-    g.iota(T.colw[:, 0:1], [[1, 1]], 0, 32, allow_small_or_imprecise_dtypes=True).then_inc(sio, 1)
     g.iota(T.rowj[:], [[1, 16], [32, 8]], 0, 0, allow_small_or_imprecise_dtypes=True).then_inc(sio, 1)
-    g.iota(T.ramp[:, 0:129], [[1, 129]], 0, 0).then_inc(sio, 1)
 
     nloc = 0
     g.wait_ge(T.sem.ldl, 16)
-    lsl = T.lnd[:, 2 * r:2 * r + 2]
-    for mask, group in ((offm, [d for d in ln_to if d in far]), (onm, [d for d in ln_to if d in near])):
-        if group:
-            g.remote_dma_fused([RemoteDMATransfer(dst_ids=[ident(d) for d in group], dma_engine_mask=mask,
-                                                  remote_sem=T.sem["la%d" % r], srcs=[lsl], dsts=[lsl for d in group])],
-                               local_sem=T.sem.loc)
-            nloc += cnt[mask]
+    for call in ln_calls(r):
+        g.remote_dma_fused([RemoteDMATransfer(dst_ids=[ident(d) for d in ds], dma_engine_mask=m,
+                                              remote_sem=T.sem["la%d" % r], srcs=[T.lnx[:]],
+                                              dsts=[T.lnd[:, 2 * r:2 * r + 2] for d in ds]) for m, ds in call],
+                           local_sem=T.sem.loc)
+        nloc += sum(ones_of(m) for m, ds in call)
     g.wait_ge(T.sem.ldx, 16)
     trs = []
-    for d in x_to:
-        mask = offm if d in far else onm
-        a = J * (r - window(d, n)[0])
-        trs.append(RemoteDMATransfer(dst_ids=[ident(d)], dma_engine_mask=mask, remote_sem=T.sem["xa%d" % r],
-                                     srcs=[T.win[:, xs]], dsts=[T.win[:, a:a + J]]))
-        nloc += cnt[mask]
+    for d in range(n):
+        if d != r and window(d, n)[0] <= r < window(d, n)[1]:
+            a = J * (r - window(d, n)[0])
+            trs.append(RemoteDMATransfer(dst_ids=[ident(d)], dma_engine_mask=x_mask(r, d), remote_sem=T.sem["xa%d" % r],
+                                         srcs=[T.win[:, xs]], dsts=[T.win[:, a:a + J]]))
+            nloc += ones_of(x_mask(r, d))
     g.remote_dma_fused(trs, local_sem=T.sem.loc)
     g.wait_ge(T.sem.loc, nloc)
 
     sms, nms = ev(), 0
-    for ap, val in ((T.ones[:], 1.0), (T.zer[:], 0.0), (T.csta[:], -float(Q * r)), (T.cstb[:], -7.5), (T.neg0[:], -0.0),
-                    (T.rhi[:], 0.0), (T.rlo[:], 0.0), (T.win[:, J * ns:J * ns + 8], 0.0)):
+    for ap, val in ((T.eight[:], 8.0), (T.semi[:], 0.5), (T.ones[:], 1.0), (T.zer[:], 0.0), (T.csta[:], -float(Q * r)),
+                    (T.cstb[:], -7.5), (T.neg0[:], -0.0), (T.rhi[:], 0.0), (T.rlo[:], 0.0),
+                    (T.win[:, J * ns:J * ns + 8], 0.0)):
         V.memset(ap, val).then_inc(sms, 1)
         nms += 1
-    V.wait_ge(sio, 4)
-    sc1, sc2, sc3, sw = ev(), ev(), ev(), ev()
+    sc1, sc2, sc4, sw, srow = ev(), ev(), ev(), ev(), ev()
+    sra = [ev() for i in range(4)]
+    V.wait_ge(sms, nms)
+    V.tensor_tensor_scan(T.rowa[:, 0:16], T.semi[:], T.semi[:], -8.0, A.add, A.add).then_inc(sra[0], 1)
+    V.tensor_tensor_scan(T.rowc[:, 0:129], T.eight[:, 0:129], T.eight[:, 0:129], -24.0, A.add, A.add).then_inc(srow, 1)
+    V.wait_ge(sra[0], 1)
+    V.tensor_copy(T.rowa[:, 16:32], T.rowa[:, 0:16]).then_inc(sra[1], 1)
+    V.wait_ge(sio, 2)
     V.tensor_scalar(T.cola[:, 0:1], T.colp[:, 0:1], 3, None, A.arith_shift_right).then_inc(sc1, 1)
-    V.tensor_scalar(T.mrow[:], T.ramp[:, 0:128], 15, None, A.bitwise_and).then_inc(sc1, 1)
-    srow = ev()
-    V.tensor_scalar(T.rowc[:, 0:129], T.ramp[:, 0:129], 16.0, -8.0, A.mult, A.add).then_inc(srow, 1)
+    V.tensor_scalar(T.colw[:, 0:1], T.colp[:, 0:1], 32.0, None, A.mult).then_inc(sc1, 1)
+    V.wait_ge(sra[1], 1)
+    V.tensor_copy(T.rowa[:, 32:64], T.rowa[:, 0:32]).then_inc(sra[2], 1)
     V.wait_ge(sc1, 2)
     V.tensor_scalar(T.colj[:, 0:1], T.cola[:, 0:1], -255.0, T.colw[:, 0:1], A.mult, A.add).then_inc(sc2, 1)
-    V.tensor_scalar(T.rowa[:], T.mrow[:], -7.0, None, A.add).then_inc(sc3, 1)
+    V.wait_ge(sra[2], 1)
+    V.tensor_copy(T.rowa[:, 64:128], T.rowa[:, 0:64]).then_inc(sra[3], 1)
     V.wait_ge(sc2, 1)
-    sc4 = ev()
     V.tensor_scalar(T.colk[:, 0:1], T.colj[:, 0:1], -16.0, None, A.add).then_inc(sc4, 1)
     V.tensor_scalar(T.wd[:], T.rowj[:], T.colj[:, 0:1], None, A.is_ge).then_inc(sw, 1)
     V.tensor_scalar(T.wup[:], T.rowj[:], -16.0, T.colj[:, 0:1], A.add, A.is_ge).then_inc(sw, 1)
     V.wait_ge(sc4, 1)
     V.tensor_scalar(T.wdn[:], T.rowj[:], T.colk[:, 0:1], -1.0, A.is_lt, A.mult).then_inc(sw, 1)
-    V.wait_ge(sms, nms)
-    V.wait_ge(sc3, 1)
+    V.wait_ge(sra[3], 1)
 
     E = T.pe[:, 0:nt]
     PE.wait_ge(sms, nms)
@@ -143,19 +173,20 @@ def rank_program(g, core, T, topo):
     PE.matmul(E, T.ones[0:1, :], T.cstb[0:1, 0:nt], False, False)
     PE.wait_ge(sw, 3)
 
-    V.wait_ge(T.sem.ldl, 16)
+    V.wait_ge(T.sem.ldo, 16)
     for s in range(nl):
         if s != r:
-            V.wait_ge(T.sem["la%d" % s], cnt[engines(s, r)])
+            V.wait_ge(T.sem["la%d" % s], ln_count(s, r))
     m64 = 1.5 * 2.0 ** 29
-    shi, slo, srh, srl = ev(), ev(), ev(), ev()
+    shi, slf, slo, srh, srl = ev(), ev(), ev(), ev(), ev()
     k = 2 * nl
     V.tensor_scalar(T.hi[:, 0:k], T.lnd[:, 0:k], m64, m64, A.add, A.subtract).then_inc(shi, 1)
+    V.tensor_copy(T.lnf[:, 0:k], T.lnd[:, 0:k]).then_inc(slf, 1)
     V.wait_ge(shi, 1)
     V.tensor_tensor(T.lo[:, 0:k], T.lnd[:, 0:k], T.hi[:, 0:k], A.subtract).then_inc(slo, 1)
     V.tensor_tensor_scan(T.rhi[:, 1:k], T.zer[:, 0:k - 1], T.hi[:, 0:k - 1], 0.0, A.add, A.add).then_inc(srh, 1)
-    V.wait_ge(slo, 1)
-    V.tensor_tensor_scan(T.rlo[:, 1:k], T.zer[:, 0:k - 1], T.lo[:, 0:k - 1], 0.0, A.add, A.add).then_inc(srl, 1)
+    V.wait_ge(slf, 1)
+    V.tensor_tensor_scan(T.rlo[:, 1:k], T.lnf[:, 0:k - 1], T.hi[:, 0:k - 1], 0.0, A.add, A.subtract).then_inc(srl, 1)
 
     lo0, hi0 = 2 * s0, 2 * s1
     sE = ev()
@@ -172,54 +203,58 @@ def rank_program(g, core, T, topo):
     m16 = 1.5 * 2.0 ** 27
     snp, s16 = ev(), ev()
     V.wait_ge(sE, 1)
-    V.tensor_scalar(T.nps[:, 0:nt], E, -1.0, None, A.mult).then_inc(snp, 1)
     V.tensor_scalar(T.e16[:, 0:nt], E, m16, m16, A.add, A.subtract).then_inc(s16, 1)
+    V.tensor_scalar(T.nps[:, 0:nt], E, -1.0, None, A.mult).then_inc(snp, 1)
     V.wait_ge(s16, 1)
     S.wait_ge(srow, 1)
     S.wait_ge(sms, nms)
     S.wait_ge(snp, 1)
-    stile = [ev() for i in range(nt)]
+    stc, sta, stb = [[ev() for i in range(nt)] for j in range(3)]
     for i in range(nt):
         b = slice(128 * i, 128 * i + 128)
-        S.activation(T.ca[:, 136 * i:136 * i + 129], T.rowc[:, 0:129], AF.Sign, bias=T.nps[:, i:i + 1]).then_inc(stile[i], 1)
-        V.tensor_scalar(T.aa[:, b], T.rowa[:], T.e16[:, i:i + 1], T.pe[:, i:i + 1], A.add, A.is_ge).then_inc(stile[i], 1)
-        V.tensor_scalar(T.ab[:, b], T.rowa[:], T.e16[:, i:i + 1], T.pe[:, i:i + 1], A.add, A.is_lt).then_inc(stile[i], 1)
+        S.activation(T.ca[:, 136 * i:136 * i + 129], T.rowc[:, 0:129], AF.Sign, bias=T.nps[:, i:i + 1]).then_inc(stc[i], 1)
+        V.tensor_scalar(T.aa[:, b], T.rowa[:], T.e16[:, i:i + 1], T.pe[:, i:i + 1], A.add, A.is_ge).then_inc(sta[i], 1)
+        V.tensor_scalar(T.ab[:, b], T.rowa[:], T.e16[:, i:i + 1], T.pe[:, i:i + 1], A.add, A.is_lt).then_inc(stb[i], 1)
 
-    spi = ev()
+    spi = [ev(), ev()]
+    pi = (T.pi0, T.pi1)
     for i in range(nt):
         b = slice(128 * i, 128 * i + 128)
-        PE.wait_ge(stile[i], 3)
-        PE.matmul(T.pi[:, 0:128], T.aa[:, b], T.ca[:, 136 * i + 1:136 * i + 129], i == 0, False)
-        last = PE.matmul(T.pi[:, 0:128], T.ab[:, b], T.ca[:, 136 * i:136 * i + 128], False, i == nt - 1)
-    last.then_inc(spi, 1)
+        PE.wait_ge(stc[i], 1)
+        PE.wait_ge(sta[i], 1)
+        for h in range(2):
+            c = 136 * i + 64 * h
+            PE.matmul(pi[h][:, 0:64], T.aa[:, b], T.ca[:, c + 1:c + 65], i == 0, False)
+        PE.wait_ge(stb[i], 1)
+        for h in range(2):
+            c = 136 * i + 64 * h
+            m = PE.matmul(pi[h][:, 0:64], T.ab[:, b], T.ca[:, c:c + 64], False, i == nt - 1)
+            if i == nt - 1:
+                m.then_inc(spi[h], 1)
 
-    V.wait_ge(spi, 1)
-    soa, sob = ev(), ev()
-    V.tensor_scalar(T.off[:, 64:128], T.pi[:, 64:128], float(128 * nt), 0.5, A.add, A.mult).then_inc(soa, 1)
-    V.tensor_scalar(T.off[:, 0:64], T.pi[:, 0:64], float(128 * nt), 0.5, A.add, A.mult).then_inc(sob, 1)
+    half = [ev(), ev()]
+    for h in range(2):
+        V.wait_ge(spi[h], 1)
+        V.tensor_scalar(T.off[:, 64 * h:64 * h + 64], pi[h][:, 0:64], float(128 * nt), 0.5, A.add, A.mult).then_inc(half[h], 1)
     for q in (V, S):
         q.wait_ge(T.sem.ldx, 16)
         for s in range(s0, s1):
             if s != r:
-                q.wait_ge(T.sem["xa%d" % s], cnt[engines(s, r)])
-    V.wait_ge(sob, 1)
-    S.wait_ge(soa, 1)
+                q.wait_ge(T.sem["xa%d" % s], ones_of(x_mask(s, r)))
+        q.wait_ge(half[0], 1)
     win = T.win[:, 0:wlen]
-    done = []
-    for c in range(2):
-        a = 512 * c
+    a = 0
+    for k, w in enumerate(BLOCKS):
+        if k == 1:
+            for q in (V, S):
+                q.wait_ge(half[1], 1)
         sv, ss = ev(), ev()
-        V.tensor_copy(T.yb[:, a:a + 512], win.indirect(T.off[:, a // 16:a // 16 + 32])).then_inc(sv, 1)
-        b = 1024 + 512 * c
-        S.activation(T.yb[:, b:b + 512], win.indirect(T.off[:, b // 16:b // 16 + 32]), AF.Identity,
+        V.tensor_copy(T.yb[:, a:a + w], win.indirect(T.off[:, a // 16:(a + w) // 16])).then_inc(sv, 1)
+        b = a + w
+        S.activation(T.yb[:, b:b + w], win.indirect(T.off[:, b // 16:(b + w) // 16]), AF.Identity,
                      bias=T.neg0[:, 0:1]).then_inc(ss, 1)
-        done.append((a, sv))
-        done.append((b, ss))
-    for a, sm in done[:3]:
-        Y.wait_ge(sm, 1)
-        Y.dma_start(T.y[:, a:a + 512], T.yb[:, a:a + 512]).then_inc(T.sem.sty, 16)
-    a, sm = done[3]
-    S.wait_ge(sm, 1)
-    S.dma_start(T.y[:, a:a + 512], T.yb[:, a:a + 512]).then_inc(T.sem.stz, 16)
-    Y.wait_ge(T.sem.sty, 48)
-    S.wait_ge(T.sem.stz, 16)
+        Y.wait_ge(sv, 1)
+        Y.wait_ge(ss, 1)
+        Y.dma_start(T.y[:, a:b + w], T.yb[:, a:b + w]).then_inc(T.sem.sty, 16)
+        a = b + w
+    Y.wait_ge(T.sem.sty, 16 * len(BLOCKS))

from concourse.bass import DstId, RemoteDMATransfer
from concourse.mybir import dt, AluOpType, AxisListType, ActivationFunctionType

J, Q = 256, 2048
NC = 56
BLOCKS = (256, 416, 352)
SCRATCH = {
    "lnx": ("dram", [128, 2], "int32"),
    "lnd": ("sbuf", [128, 8], "int32"),
    "lnf": ("sbuf", [128, 8], "float32"),
    "win": ("sbuf", [128, 3 * J + 8], "bfloat16"),
    "off": ("sbuf", [128, Q // 16], "uint16"),
    "yb": ("sbuf", [128, Q], "bfloat16"),
    "colp": ("sbuf", [128, 4], "int32"),
    "cola": ("sbuf", [128, 4], "int32"),
    "colw": ("sbuf", [128, 4], "float32"),
    "colj": ("sbuf", [128, 4], "float32"),
    "colk": ("sbuf", [128, 4], "float32"),
    "rowj": ("sbuf", [128, 128], "bfloat16"),
    "rowc": ("sbuf", [128, 136], "bfloat16"),
    "rowa": ("sbuf", [128, 128], "bfloat16"),
    "eight": ("sbuf", [128, 136], "bfloat16"),
    "semi": ("sbuf", [128, 16], "bfloat16"),
    "wd": ("sbuf", [128, 128], "bfloat16"),
    "wup": ("sbuf", [128, 128], "bfloat16"),
    "wdn": ("sbuf", [128, 128], "bfloat16"),
    "ones": ("sbuf", [128, 128], "bfloat16"),
    "zer": ("sbuf", [128, 8], "bfloat16"),
    "csta": ("sbuf", [128, 8], "bfloat16"),
    "cstb": ("sbuf", [128, 8], "bfloat16"),
    "neg0": ("sbuf", [128, 4], "float32"),
    "hi": ("sbuf", [128, 8], "bfloat16"),
    "lo": ("sbuf", [128, 8], "bfloat16"),
    "rhi": ("sbuf", [128, 16], "bfloat16"),
    "rlo": ("sbuf", [128, 16], "bfloat16"),
    "nps": ("sbuf", [128, 8], "float32"),
    "e16": ("sbuf", [128, 8], "float32"),
    "ca": ("sbuf", [128, 6 * 136], "bfloat16"),
    "aa": ("sbuf", [128, 6 * 128], "bfloat16"),
    "ab": ("sbuf", [128, 6 * 128], "bfloat16"),
    "pe": ("psum", [128, 512], "float32"),
    "pi0": ("psum", [128, 512], "float32"),
    "pi1": ("psum", [128, 512], "float32"),
}
SEMAPHORES = (["ldl", "ldo", "ldx", "loc", "sty"] + ["la%d" % s for s in range(4)] + ["xa%d" % s for s in range(4)]
              + ["e%d" % k for k in range(NC)])


def window(r, n):
    return max(0, r - 1), min(n, r + 2)


def ln_dests(r, n):
    ds = [d for d in range(n) if d != r and r < window(d, n)[1]]
    size = {d: window(d, n)[1] - window(d, n)[0] for d in range(n)}
    top = max(size.values())
    return [d for d in ds if size[d] == top], [d for d in ds if size[d] < top]


def rank_program(g, core, T, topo):
    r = T.rank_of(core)
    if r is None:
        return
    n = len(T.cores)
    A = AluOpType
    AF = ActivationFunctionType
    V, S, PE, Y = g.vector, g.scalar, g.tensor, g.sync
    s0, s1 = window(r, n)
    ns, nl = s1 - s0, s1
    nt = 2 * ns
    wlen = J * ns + 8
    used = [0]

    def ev():
        used[0] += 1
        return T.sem["e%d" % (used[0] - 1)]

    xs = slice(J * (r - s0), J * (r - s0) + J)
    Y.dma_start(T.lnx[:], T.ln[:]).then_inc(T.sem.ldl, 16)
    Y.dma_start(T.win[:, xs], T.x[:]).then_inc(T.sem.ldx, 16)
    Y.dma_start(T.lnd[:, 2 * r:2 * r + 2], T.ln[:]).then_inc(T.sem.ldo, 16)

    def is_near(a, b):
        a, b = T.cores[a], T.cores[b]
        return topo.host(a) == topo.host(b) and topo.chip(a) == topo.chip(b)

    def masks(s):
        far = [d for d in range(n) if not is_near(s, d)][0]
        near = [d for d in range(n) if d != s and is_near(s, d)][0]
        m = topo.mask(T.cores[s], T.cores[far])
        return m, topo.mask(T.cores[s], T.cores[near]) & ~m

    def ln_calls(s):
        offm, onm = masks(s)
        first, rest = ln_dests(s, n)
        calls = []
        fars = [d for d in first if not is_near(s, d)]
        nears = [d for d in first if is_near(s, d)]
        calls.append([(offm if fars else onm, fars + nears)])
        calls.append([(m, ds) for m, ds in ((offm, [d for d in rest if not is_near(s, d)]),
                                            (onm, [d for d in rest if is_near(s, d)])) if ds])
        return [c for c in calls if c]

    def ones_of(m):
        return bin(m).count("1")

    def ln_count(s, d):
        return [ones_of(m) for c in ln_calls(s) for m, ds in c if d in ds][0]

    def x_mask(s, d):
        return masks(s)[1 if is_near(s, d) else 0]

    def ident(d):
        rid, pid = topo.addr(T.cores[d], core)
        return DstId(rid=rid, pnc=pid)

    sio = ev()
    g.iota(T.colp[:, 0:1], [[1, 1]], 0, 1).then_inc(sio, 1)
    g.iota(T.rowj[:], [[1, 16], [32, 8]], 0, 0, allow_small_or_imprecise_dtypes=True).then_inc(sio, 1)

    nloc = 0
    g.wait_ge(T.sem.ldl, 16)
    for call in ln_calls(r):
        g.remote_dma_fused([RemoteDMATransfer(dst_ids=[ident(d) for d in ds], dma_engine_mask=m,
                                              remote_sem=T.sem["la%d" % r], srcs=[T.lnx[:]],
                                              dsts=[T.lnd[:, 2 * r:2 * r + 2] for d in ds]) for m, ds in call],
                           local_sem=T.sem.loc)
        nloc += sum(ones_of(m) for m, ds in call)
    g.wait_ge(T.sem.ldx, 16)
    trs = []
    for d in range(n):
        if d != r and window(d, n)[0] <= r < window(d, n)[1]:
            a = J * (r - window(d, n)[0])
            trs.append(RemoteDMATransfer(dst_ids=[ident(d)], dma_engine_mask=x_mask(r, d), remote_sem=T.sem["xa%d" % r],
                                         srcs=[T.win[:, xs]], dsts=[T.win[:, a:a + J]]))
            nloc += ones_of(x_mask(r, d))
    g.remote_dma_fused(trs, local_sem=T.sem.loc)
    g.wait_ge(T.sem.loc, nloc)

    sms, nms = ev(), 0
    for ap, val in ((T.eight[:], 8.0), (T.semi[:], 0.5), (T.ones[:], 1.0), (T.zer[:], 0.0), (T.csta[:], -float(Q * r)),
                    (T.cstb[:], -7.5), (T.neg0[:], -0.0), (T.rhi[:], 0.0), (T.rlo[:], 0.0),
                    (T.win[:, J * ns:J * ns + 8], 0.0)):
        V.memset(ap, val).then_inc(sms, 1)
        nms += 1
    sc1, sc2, sc4, sw, srow = ev(), ev(), ev(), ev(), ev()
    sra = [ev() for i in range(4)]
    V.wait_ge(sms, nms)
    V.tensor_tensor_scan(T.rowa[:, 0:16], T.semi[:], T.semi[:], -8.0, A.add, A.add).then_inc(sra[0], 1)
    V.tensor_tensor_scan(T.rowc[:, 0:129], T.eight[:, 0:129], T.eight[:, 0:129], -24.0, A.add, A.add).then_inc(srow, 1)
    V.wait_ge(sra[0], 1)
    V.tensor_copy(T.rowa[:, 16:32], T.rowa[:, 0:16]).then_inc(sra[1], 1)
    V.wait_ge(sio, 2)
    V.tensor_scalar(T.cola[:, 0:1], T.colp[:, 0:1], 3, None, A.arith_shift_right).then_inc(sc1, 1)
    V.tensor_scalar(T.colw[:, 0:1], T.colp[:, 0:1], 32.0, None, A.mult).then_inc(sc1, 1)
    V.wait_ge(sra[1], 1)
    V.tensor_copy(T.rowa[:, 32:64], T.rowa[:, 0:32]).then_inc(sra[2], 1)
    V.wait_ge(sc1, 2)
    V.tensor_scalar(T.colj[:, 0:1], T.cola[:, 0:1], -255.0, T.colw[:, 0:1], A.mult, A.add).then_inc(sc2, 1)
    V.wait_ge(sra[2], 1)
    V.tensor_copy(T.rowa[:, 64:128], T.rowa[:, 0:64]).then_inc(sra[3], 1)
    V.wait_ge(sc2, 1)
    V.tensor_scalar(T.colk[:, 0:1], T.colj[:, 0:1], -16.0, None, A.add).then_inc(sc4, 1)
    V.tensor_scalar(T.wd[:], T.rowj[:], T.colj[:, 0:1], None, A.is_ge).then_inc(sw, 1)
    V.tensor_scalar(T.wup[:], T.rowj[:], -16.0, T.colj[:, 0:1], A.add, A.is_ge).then_inc(sw, 1)
    V.wait_ge(sc4, 1)
    V.tensor_scalar(T.wdn[:], T.rowj[:], T.colk[:, 0:1], -1.0, A.is_lt, A.mult).then_inc(sw, 1)
    V.wait_ge(sra[3], 1)

    E = T.pe[:, 0:nt]
    PE.wait_ge(sms, nms)
    PE.matmul(E, T.ones[0:1, :], T.csta[0:1, 0:nt], True, False)
    PE.matmul(E, T.ones[0:1, :], T.cstb[0:1, 0:nt], False, False)
    PE.wait_ge(sw, 3)

    V.wait_ge(T.sem.ldo, 16)
    for s in range(nl):
        if s != r:
            V.wait_ge(T.sem["la%d" % s], ln_count(s, r))
    m64 = 1.5 * 2.0 ** 29
    shi, slf, slo, srh, srl = ev(), ev(), ev(), ev(), ev()
    k = 2 * nl
    V.tensor_scalar(T.hi[:, 0:k], T.lnd[:, 0:k], m64, m64, A.add, A.subtract).then_inc(shi, 1)
    V.tensor_copy(T.lnf[:, 0:k], T.lnd[:, 0:k]).then_inc(slf, 1)
    V.wait_ge(shi, 1)
    V.tensor_tensor(T.lo[:, 0:k], T.lnd[:, 0:k], T.hi[:, 0:k], A.subtract).then_inc(slo, 1)
    V.tensor_tensor_scan(T.rhi[:, 1:k], T.zer[:, 0:k - 1], T.hi[:, 0:k - 1], 0.0, A.add, A.add).then_inc(srh, 1)
    V.wait_ge(slf, 1)
    V.tensor_tensor_scan(T.rlo[:, 1:k], T.lnf[:, 0:k - 1], T.hi[:, 0:k - 1], 0.0, A.add, A.subtract).then_inc(srl, 1)

    lo0, hi0 = 2 * s0, 2 * s1
    sE = ev()
    for sm, t in ((shi, T.hi), (slo, T.lo)):
        PE.wait_ge(sm, 1)
        PE.matmul(E, T.wd[:], t[:, lo0:hi0], False, False)
        PE.matmul(T.pe[:, 0:nt:2], T.wup[:], t[:, lo0 + 1:hi0:2], False, False)
        PE.matmul(T.pe[:, 1:nt:2], T.wdn[:], t[:, lo0:hi0:2], False, False)
    PE.wait_ge(srh, 1)
    PE.matmul(E, T.ones[:], T.rhi[:, lo0:hi0], False, False)
    PE.wait_ge(srl, 1)
    PE.matmul(E, T.ones[:], T.rlo[:, lo0:hi0], False, True).then_inc(sE, 1)

    m16 = 1.5 * 2.0 ** 27
    snp, s16 = ev(), ev()
    V.wait_ge(sE, 1)
    V.tensor_scalar(T.e16[:, 0:nt], E, m16, m16, A.add, A.subtract).then_inc(s16, 1)
    V.tensor_scalar(T.nps[:, 0:nt], E, -1.0, None, A.mult).then_inc(snp, 1)
    V.wait_ge(s16, 1)
    S.wait_ge(srow, 1)
    S.wait_ge(sms, nms)
    S.wait_ge(snp, 1)
    stc, sta, stb = [[ev() for i in range(nt)] for j in range(3)]
    for i in range(nt):
        b = slice(128 * i, 128 * i + 128)
        S.activation(T.ca[:, 136 * i:136 * i + 129], T.rowc[:, 0:129], AF.Sign, bias=T.nps[:, i:i + 1]).then_inc(stc[i], 1)
        V.tensor_scalar(T.aa[:, b], T.rowa[:], T.e16[:, i:i + 1], T.pe[:, i:i + 1], A.add, A.is_ge).then_inc(sta[i], 1)
        V.tensor_scalar(T.ab[:, b], T.rowa[:], T.e16[:, i:i + 1], T.pe[:, i:i + 1], A.add, A.is_lt).then_inc(stb[i], 1)

    spi = [ev(), ev()]
    pi = (T.pi0, T.pi1)
    for i in range(nt):
        b = slice(128 * i, 128 * i + 128)
        PE.wait_ge(stc[i], 1)
        PE.wait_ge(sta[i], 1)
        for h in range(2):
            c = 136 * i + 64 * h
            PE.matmul(pi[h][:, 0:64], T.aa[:, b], T.ca[:, c + 1:c + 65], i == 0, False)
        PE.wait_ge(stb[i], 1)
        for h in range(2):
            c = 136 * i + 64 * h
            m = PE.matmul(pi[h][:, 0:64], T.ab[:, b], T.ca[:, c:c + 64], False, i == nt - 1)
            if i == nt - 1:
                m.then_inc(spi[h], 1)

    half = [ev(), ev()]
    for h in range(2):
        V.wait_ge(spi[h], 1)
        V.tensor_scalar(T.off[:, 64 * h:64 * h + 64], pi[h][:, 0:64], float(128 * nt), 0.5, A.add, A.mult).then_inc(half[h], 1)
    for q in (V, S):
        q.wait_ge(T.sem.ldx, 16)
        for s in range(s0, s1):
            if s != r:
                q.wait_ge(T.sem["xa%d" % s], ones_of(x_mask(s, r)))
        q.wait_ge(half[0], 1)
    win = T.win[:, 0:wlen]
    a = 0
    for k, w in enumerate(BLOCKS):
        if k == 1:
            for q in (V, S):
                q.wait_ge(half[1], 1)
        sv, ss = ev(), ev()
        V.tensor_copy(T.yb[:, a:a + w], win.indirect(T.off[:, a // 16:(a + w) // 16])).then_inc(sv, 1)
        b = a + w
        S.activation(T.yb[:, b:b + w], win.indirect(T.off[:, b // 16:(b + w) // 16]), AF.Identity,
                     bias=T.neg0[:, 0:1]).then_inc(ss, 1)
        Y.wait_ge(sv, 1)
        Y.wait_ge(ss, 1)
        Y.dma_start(T.y[:, a:b + w], T.yb[:, a:b + w]).then_inc(T.sem.sty, 16)
        a = b + w
    Y.wait_ge(T.sem.sty, 16 * len(BLOCKS))
